import numpy as np, ml_dtypes
CORES = [242,247,114,119]
N = 4
import mx_ref
NC = 256
CNT = [[24,40,32,160],[48,0,144,64],[184,32,40,0],[0,184,40,32]]
OFF = [[sum(c[:e]) for e in range(N + 1)] for c in CNT]
BF = ml_dtypes.bfloat16
def setup_inputs(rng):
    def f(*shape):
        return mx_ref.flush((rng.standard_normal(shape, dtype=np.float32) * np.exp2(rng.integers(-2, 3, shape[:-1] + (1,)))).astype(BF))
    return {"w": f(N, 128, 512), "x": f(N, 128, 4 * NC)}
def setup_inputs_blocks(rng):
    d = setup_inputs(rng)
    for k in ("w", "x"): d[k] = mx_ref.spread(d[k], rng, 4)
    return d
def setup_inputs_wide(rng):
    d = setup_inputs(rng)
    for k in ("w", "x"): d[k] = mx_ref.flush((d[k].astype(np.float32) * np.exp2(rng.integers(-8, 9, (N, 1, 1))).astype(np.float32)).astype(BF))
    return d
def setup_inputs_zeros(rng):
    d = setup_inputs(rng); v = d["x"].reshape(N, 128, -1, 4).copy()
    v[np.broadcast_to((rng.random((N, 1, v.shape[2], 1)) < 0.33), v.shape)] = 0
    d["x"] = v.reshape(d["x"].shape)
    return d
def reference(w, x):
    y = np.zeros((N, 128, NC), np.float32)
    for e in range(N):
        t = np.concatenate([x[j][:, 4 * OFF[j][e]:4 * OFF[j][e + 1]] for j in range(N)], axis=1)
        p = mx_ref.matmul(mx_ref.quantize(w[e]), mx_ref.quantize(t)); c = 0
        for j in range(N):
            a, b = OFF[j][e], OFF[j][e + 1]
            y[j][:, a:b] = p[:, c:c + b - a]; c += b - a
    return {"y": y}

@@ -1,0 +1,108 @@
+from concourse.bass import DstId, RemoteDMATransfer
+from concourse.mybir import dt, ActivationFunctionType
+
+NR = 4
+WC = 128
+XC = 256
+LEAST = 128
+BANK = 512
+
+SCRATCH = {
+    "wb": ("sbuf", [128, 4 * WC], "bfloat16"),
+    "xb": ("sbuf", [128, 4 * XC], "bfloat16"),
+    "wc": ("sbuf", [128, NR * WC], "float8_e4m3fn_x4"),
+    "ws": ("sbuf", [128, NR * WC], "uint8"),
+    "xc": ("sbuf", [128, XC], "float8_e4m3fn_x4"),
+    "xs": ("sbuf", [128, XC], "uint8"),
+    "ps": ("psum", [128, NR * BANK], "float32"),
+    "yb": ("sbuf", [128, XC], "float32"),
+}
+SEMAPHORES = ["lw", "lx", "qw", "qx", "arr0", "arr1", "arr2", "arr3", "mm0", "mm1", "mm2", "mm3", "cp", "st", "left"]
+
+
+def _engines(mask):
+    return bin(mask).count("1")
+
+
+def rank_program(g, core, T, topo):
+    rank = T.rank_of(core)
+    if rank is None:
+        return
+    cores, cnt, sem = T.cores, T.tables["CNT"], T.sem
+    n = len(cores)
+
+    def same_chip(a, b):
+        return topo.host(a) == topo.host(b) and topo.chip(a) == topo.chip(b)
+
+    def plan(e):
+        src = cores[e]
+        takers = [j for j in range(n) if j != e and cnt[j][e] > 0]
+        groups, used = [], 0
+        for near in (False, True):
+            js = [j for j in takers if same_chip(src, cores[j]) == near]
+            if not js:
+                continue
+            m = topo.mask(src, cores[js[0]])
+            for j in js:
+                m &= topo.mask(src, cores[j])
+            if m & ~used:
+                m &= ~used
+            groups.append((js, m))
+            used |= m
+        return groups
+
+    def slot(e):
+        return slice(e * WC, (e + 1) * WC)
+
+    g.sync.dma_start(T.wb[:], T.w[:]).then_inc(sem.lw, 16)
+    g.sync.dma_start(T.xb[:], T.x[:]).then_inc(sem.lx, 16)
+    g.vector.wait_ge(sem.lw, 16)
+    g.vector.quantize_mx(T.wc[:, slot(rank)], T.ws[:, slot(rank)], T.wb[:]).then_inc(sem.qw, 1)
+    g.vector.wait_ge(sem.lx, 16)
+    g.vector.quantize_mx(T.xc[:], T.xs[:], T.xb[:]).then_inc(sem.qx, 1)
+
+    g.wait_ge(sem.qw, 1)
+    left = 0
+    for js, m in plan(rank):
+        ids = []
+        for j in js:
+            rid, pid = topo.addr(cores[j], core)
+            ids.append(DstId(rid=rid, pnc=pid))
+        for view in (T.wc[:, slot(rank)].bitcast(dt.uint8), T.ws[:, slot(rank)]):
+            g.remote_dma_fused(
+                [RemoteDMATransfer(dst_ids=ids, dma_engine_mask=m, remote_sem=sem["arr%d" % rank],
+                                   srcs=[view], dsts=[view] * len(js), alu_op=0)],
+                local_sem=sem.left)
+            left += _engines(m)
+
+    def due(e):
+        if e == rank:
+            return 0, 0
+        for js, m in plan(e):
+            if rank in js:
+                return (1 if same_chip(cores[e], core) else 1 + len(js)), 2 * _engines(m)
+
+    mine = sorted((e for e in range(n) if cnt[rank][e] > 0), key=lambda e: (due(e)[0], -cnt[rank][e]))
+    g.tensor.wait_ge(sem.qx, 1)
+    for k, e in enumerate(mine):
+        c, a = cnt[rank][e], sum(cnt[rank][:e])
+        wide = max(c, LEAST)
+        lo = min(a, XC - wide)
+        if e == rank:
+            g.tensor.wait_ge(sem.qw, 1)
+        else:
+            g.tensor.wait_ge(sem["arr%d" % e], due(e)[1])
+        g.tensor.matmul_mx(T.ps[:, k * BANK:k * BANK + wide], T.wc[:, slot(e)], T.ws[:, slot(e)],
+                           T.xc[:, lo:lo + wide], T.xs[:, lo:lo + wide], True, True).then_inc(sem["mm%d" % e], 1)
+        got = T.ps[:, k * BANK + a - lo:k * BANK + a - lo + c]
+        if (len(mine) - 1 - k) % 2 == 0:
+            g.vector.wait_ge(sem["mm%d" % e], 1)
+            g.vector.tensor_copy(T.yb[:, a:a + c], got).then_inc(sem.cp, 1)
+        else:
+            g.scalar.wait_ge(sem["mm%d" % e], 1)
+            g.scalar.activation(T.yb[:, a:a + c], got, ActivationFunctionType.Copy).then_inc(sem.cp, 1)
+
+    g.sync.wait_ge(sem.cp, len(mine))
+    g.sync.dma_start(T.y[:], T.yb[:]).then_inc(sem.st, 16)
+    g.sync.wait_ge(sem.st, 16)
+    g.wait_ge(sem.left, left)

@@ -1,4 +1,3 @@
-from concourse.bass import DstId, RemoteDMATransfer
 from concourse.mybir import dt, ActivationFunctionType
 
 NR = 4
@@ -6,6 +5,7 @@ WC = 128
 XC = 256
 LEAST = 128
 BANK = 512
+FRESH = 4
 
 SCRATCH = {
     "wb": ("sbuf", [128, 4 * WC], "bfloat16"),
@@ -17,11 +17,18 @@ SCRATCH = {
     "ps": ("psum", [128, NR * BANK], "float32"),
     "yb": ("sbuf", [128, XC], "float32"),
 }
-SEMAPHORES = ["lw", "lx", "qw", "qx", "arr0", "arr1", "arr2", "arr3", "mm0", "mm1", "mm2", "mm3", "cp", "st", "left"]
+SEMAPHORES = ["lw", "lx", "qw", "qx", "arr0", "arr1", "arr2", "arr3", "sc0", "sc1", "sc2", "sc3",
+              "mm0", "mm1", "mm2", "mm3", "cp0", "cp1", "cp2", "cp3", "st", "left"]
+
+OWN, EARLY, NEAR, LAST = 0, 1, 2, 3
 
 
 def _engines(mask):
     return bin(mask).count("1")
+
+
+def _lowest(mask, k):
+    return sum(1 << b for b in [b for b in range(16) if mask >> b & 1][:k])
 
 
 def rank_program(g, core, T, topo):
@@ -34,22 +41,45 @@ def rank_program(g, core, T, topo):
     def same_chip(a, b):
         return topo.host(a) == topo.host(b) and topo.chip(a) == topo.chip(b)
 
-    def plan(e):
-        src = cores[e]
-        takers = [j for j in range(n) if j != e and cnt[j][e] > 0]
-        groups, used = [], 0
-        for near in (False, True):
-            js = [j for j in takers if same_chip(src, cores[j]) == near]
-            if not js:
-                continue
-            m = topo.mask(src, cores[js[0]])
-            for j in js:
-                m &= topo.mask(src, cores[j])
-            if m & ~used:
-                m &= ~used
-            groups.append((js, m))
-            used |= m
-        return groups
+    def takers(e):
+        js = [j for j in range(n) if j != e and cnt[j][e] > 0]
+        far = sorted((j for j in js if not same_chip(cores[e], cores[j])), key=lambda j: -cnt[j][e])
+        return far, [j for j in js if same_chip(cores[e], cores[j])]
+
+    def passed(e):
+        far, _ = takers(e)
+        return [j for j in far[1:] if same_chip(cores[j], cores[far[0]])]
+
+    def stays(r, j):
+        m = topo.mask(cores[r], cores[j])
+        for k in takers(r)[0]:
+            if m & ~topo.mask(cores[r], cores[k]):
+                m &= ~topo.mask(cores[r], cores[k])
+        return m
+
+    def calls(e):
+        far, near = takers(e)
+        out = []
+        for j in far:
+            m = topo.mask(cores[e], cores[j])
+            out += [(True, j, m)] if j in passed(e) else [(False, j, m), (True, j, m)]
+        for j in near:
+            out += [(False, j, stays(e, j)), (True, j, stays(e, j))]
+        return out
+
+    def passes(r):
+        out = []
+        for e in range(n):
+            if e != r and takers(e)[0][:1] == [r]:
+                for j in passed(e):
+                    m = stays(r, j)
+                    out.append((e, j, m if takers(r)[1] else _lowest(m, FRESH)))
+        return out
+
+    def lands(e, codes):
+        if not codes and rank in passed(e):
+            return sum(_engines(m) for x, j, m in passes(takers(e)[0][0]) if x == e and j == rank)
+        return sum(_engines(m) for c, j, m in calls(e) if j == rank and c == codes)
 
     def slot(e):
         return slice(e * WC, (e + 1) * WC)
@@ -63,46 +93,73 @@ def rank_program(g, core, T, topo):
 
     g.wait_ge(sem.qw, 1)
     left = 0
-    for js, m in plan(rank):
-        ids = []
-        for j in js:
-            rid, pid = topo.addr(cores[j], core)
-            ids.append(DstId(rid=rid, pnc=pid))
-        for view in (T.wc[:, slot(rank)].bitcast(dt.uint8), T.ws[:, slot(rank)]):
-            g.remote_dma_fused(
-                [RemoteDMATransfer(dst_ids=ids, dma_engine_mask=m, remote_sem=sem["arr%d" % rank],
-                                   srcs=[view], dsts=[view] * len(js), alu_op=0)],
-                local_sem=sem.left)
-            left += _engines(m)
+    for codes, j, m in calls(rank):
+        view = T.wc[:, slot(rank)].bitcast(dt.uint8) if codes else T.ws[:, slot(rank)]
+        rid, pid = topo.addr(cores[j], core)
+        g.remote_dma(view, view, sem[("arr%d" if codes else "sc%d") % rank], sem.left, pid, rid, m)
+        left += _engines(m)
+    for e, j, m in passes(rank):
+        g.wait_ge(sem["sc%d" % e], lands(e, False))
+        rid, pid = topo.addr(cores[j], core)
+        g.remote_dma(T.ws[:, slot(e)], T.ws[:, slot(e)], sem["sc%d" % e], sem.left, pid, rid, m)
+        left += _engines(m)
 
     def due(e):
         if e == rank:
-            return 0, 0
-        for js, m in plan(e):
-            if rank in js:
-                return (1 if same_chip(cores[e], core) else 1 + len(js)), 2 * _engines(m)
+            return OWN
+        far, near = takers(e)
+        if rank in near:
+            return NEAR
+        return LAST if len(far) > 1 and far[-1] == rank else EARLY
 
-    mine = sorted((e for e in range(n) if cnt[rank][e] > 0), key=lambda e: (due(e)[0], -cnt[rank][e]))
+    mine = sorted((e for e in range(n) if cnt[rank][e] > 0), key=lambda e: (due(e), -cnt[rank][e]))
+    first = {e: sum(cnt[rank][:e]) for e in mine}
+
     g.tensor.wait_ge(sem.qx, 1)
     for k, e in enumerate(mine):
-        c, a = cnt[rank][e], sum(cnt[rank][:e])
+        c, a = cnt[rank][e], first[e]
         wide = max(c, LEAST)
         lo = min(a, XC - wide)
         if e == rank:
             g.tensor.wait_ge(sem.qw, 1)
         else:
-            g.tensor.wait_ge(sem["arr%d" % e], due(e)[1])
+            g.tensor.wait_ge(sem["sc%d" % e], lands(e, False))
+            g.tensor.wait_ge(sem["arr%d" % e], lands(e, True))
         g.tensor.matmul_mx(T.ps[:, k * BANK:k * BANK + wide], T.wc[:, slot(e)], T.ws[:, slot(e)],
                            T.xc[:, lo:lo + wide], T.xs[:, lo:lo + wide], True, True).then_inc(sem["mm%d" % e], 1)
-        got = T.ps[:, k * BANK + a - lo:k * BANK + a - lo + c]
-        if (len(mine) - 1 - k) % 2 == 0:
-            g.vector.wait_ge(sem["mm%d" % e], 1)
-            g.vector.tensor_copy(T.yb[:, a:a + c], got).then_inc(sem.cp, 1)
-        else:
-            g.scalar.wait_ge(sem["mm%d" % e], 1)
-            g.scalar.activation(T.yb[:, a:a + c], got, ActivationFunctionType.Copy).then_inc(sem.cp, 1)
 
-    g.sync.wait_ge(sem.cp, len(mine))
-    g.sync.dma_start(T.y[:], T.yb[:]).then_inc(sem.st, 16)
-    g.sync.wait_ge(sem.st, 16)
+    def copy(e):
+        k, c, a = mine.index(e), cnt[rank][e], first[e]
+        lo = min(a, XC - max(c, LEAST))
+        got = T.ps[:, k * BANK + a - lo:k * BANK + a - lo + c]
+        if due(e) == NEAR:
+            g.scalar.wait_ge(sem["mm%d" % e], 1)
+            g.scalar.activation(T.yb[:, a:a + c], got, ActivationFunctionType.Copy).then_inc(sem["cp%d" % e], 1)
+        else:
+            g.vector.wait_ge(sem["mm%d" % e], 1)
+            g.vector.tensor_copy(T.yb[:, a:a + c], got).then_inc(sem["cp%d" % e], 1)
+
+    def store(q, run):
+        for e in run:
+            q.wait_ge(sem["cp%d" % e], 1)
+        a, b = first[run[0]], first[run[-1]] + cnt[rank][run[-1]]
+        q.dma_start(T.y[:, a:b], T.yb[:, a:b]).then_inc(sem.st, 16)
+
+    runs = []
+    for e in sorted(mine):
+        if runs and due(e) != EARLY and due(runs[-1][-1]) != EARLY:
+            runs[-1].append(e)
+        else:
+            runs.append([e])
+    runs.sort(key=lambda run: max(due(e) for e in run))
+
+    for e in mine:
+        if due(e) != NEAR:
+            copy(e)
+    for run in runs:
+        for e in run:
+            if due(e) == NEAR:
+                copy(e)
+        store(g.sync if run is runs[-1] else g.scalar, run)
+    g.sync.wait_ge(sem.st, 16 * len(runs))
     g.wait_ge(sem.left, left)

from concourse.mybir import dt, ActivationFunctionType

NR = 4
WC = 128
XC = 256
LEAST = 128
BANK = 512
FRESH = 4

SCRATCH = {
    "wb": ("sbuf", [128, 4 * WC], "bfloat16"),
    "xb": ("sbuf", [128, 4 * XC], "bfloat16"),
    "wc": ("sbuf", [128, NR * WC], "float8_e4m3fn_x4"),
    "ws": ("sbuf", [128, NR * WC], "uint8"),
    "xc": ("sbuf", [128, XC], "float8_e4m3fn_x4"),
    "xs": ("sbuf", [128, XC], "uint8"),
    "ps": ("psum", [128, NR * BANK], "float32"),
    "yb": ("sbuf", [128, XC], "float32"),
}
SEMAPHORES = ["lw", "lx", "qw", "qx", "arr0", "arr1", "arr2", "arr3", "sc0", "sc1", "sc2", "sc3",
              "mm0", "mm1", "mm2", "mm3", "cp0", "cp1", "cp2", "cp3", "st", "left"]

OWN, EARLY, NEAR, LAST = 0, 1, 2, 3


def _engines(mask):
    return bin(mask).count("1")


def _lowest(mask, k):
    return sum(1 << b for b in [b for b in range(16) if mask >> b & 1][:k])


def rank_program(g, core, T, topo):
    rank = T.rank_of(core)
    if rank is None:
        return
    cores, cnt, sem = T.cores, T.tables["CNT"], T.sem
    n = len(cores)

    def same_chip(a, b):
        return topo.host(a) == topo.host(b) and topo.chip(a) == topo.chip(b)

    def takers(e):
        js = [j for j in range(n) if j != e and cnt[j][e] > 0]
        far = sorted((j for j in js if not same_chip(cores[e], cores[j])), key=lambda j: -cnt[j][e])
        return far, [j for j in js if same_chip(cores[e], cores[j])]

    def passed(e):
        far, _ = takers(e)
        return [j for j in far[1:] if same_chip(cores[j], cores[far[0]])]

    def stays(r, j):
        m = topo.mask(cores[r], cores[j])
        for k in takers(r)[0]:
            if m & ~topo.mask(cores[r], cores[k]):
                m &= ~topo.mask(cores[r], cores[k])
        return m

    def calls(e):
        far, near = takers(e)
        out = []
        for j in far:
            m = topo.mask(cores[e], cores[j])
            out += [(True, j, m)] if j in passed(e) else [(False, j, m), (True, j, m)]
        for j in near:
            out += [(False, j, stays(e, j)), (True, j, stays(e, j))]
        return out

    def passes(r):
        out = []
        for e in range(n):
            if e != r and takers(e)[0][:1] == [r]:
                for j in passed(e):
                    m = stays(r, j)
                    out.append((e, j, m if takers(r)[1] else _lowest(m, FRESH)))
        return out

    def lands(e, codes):
        if not codes and rank in passed(e):
            return sum(_engines(m) for x, j, m in passes(takers(e)[0][0]) if x == e and j == rank)
        return sum(_engines(m) for c, j, m in calls(e) if j == rank and c == codes)

    def slot(e):
        return slice(e * WC, (e + 1) * WC)

    g.sync.dma_start(T.wb[:], T.w[:]).then_inc(sem.lw, 16)
    g.sync.dma_start(T.xb[:], T.x[:]).then_inc(sem.lx, 16)
    g.vector.wait_ge(sem.lw, 16)
    g.vector.quantize_mx(T.wc[:, slot(rank)], T.ws[:, slot(rank)], T.wb[:]).then_inc(sem.qw, 1)
    g.vector.wait_ge(sem.lx, 16)
    g.vector.quantize_mx(T.xc[:], T.xs[:], T.xb[:]).then_inc(sem.qx, 1)

    g.wait_ge(sem.qw, 1)
    left = 0
    for codes, j, m in calls(rank):
        view = T.wc[:, slot(rank)].bitcast(dt.uint8) if codes else T.ws[:, slot(rank)]
        rid, pid = topo.addr(cores[j], core)
        g.remote_dma(view, view, sem[("arr%d" if codes else "sc%d") % rank], sem.left, pid, rid, m)
        left += _engines(m)
    for e, j, m in passes(rank):
        g.wait_ge(sem["sc%d" % e], lands(e, False))
        rid, pid = topo.addr(cores[j], core)
        g.remote_dma(T.ws[:, slot(e)], T.ws[:, slot(e)], sem["sc%d" % e], sem.left, pid, rid, m)
        left += _engines(m)

    def due(e):
        if e == rank:
            return OWN
        far, near = takers(e)
        if rank in near:
            return NEAR
        return LAST if len(far) > 1 and far[-1] == rank else EARLY

    mine = sorted((e for e in range(n) if cnt[rank][e] > 0), key=lambda e: (due(e), -cnt[rank][e]))
    first = {e: sum(cnt[rank][:e]) for e in mine}

    g.tensor.wait_ge(sem.qx, 1)
    for k, e in enumerate(mine):
        c, a = cnt[rank][e], first[e]
        wide = max(c, LEAST)
        lo = min(a, XC - wide)
        if e == rank:
            g.tensor.wait_ge(sem.qw, 1)
        else:
            g.tensor.wait_ge(sem["sc%d" % e], lands(e, False))
            g.tensor.wait_ge(sem["arr%d" % e], lands(e, True))
        g.tensor.matmul_mx(T.ps[:, k * BANK:k * BANK + wide], T.wc[:, slot(e)], T.ws[:, slot(e)],
                           T.xc[:, lo:lo + wide], T.xs[:, lo:lo + wide], True, True).then_inc(sem["mm%d" % e], 1)

    def copy(e):
        k, c, a = mine.index(e), cnt[rank][e], first[e]
        lo = min(a, XC - max(c, LEAST))
        got = T.ps[:, k * BANK + a - lo:k * BANK + a - lo + c]
        if due(e) == NEAR:
            g.scalar.wait_ge(sem["mm%d" % e], 1)
            g.scalar.activation(T.yb[:, a:a + c], got, ActivationFunctionType.Copy).then_inc(sem["cp%d" % e], 1)
        else:
            g.vector.wait_ge(sem["mm%d" % e], 1)
            g.vector.tensor_copy(T.yb[:, a:a + c], got).then_inc(sem["cp%d" % e], 1)

    def store(q, run):
        for e in run:
            q.wait_ge(sem["cp%d" % e], 1)
        a, b = first[run[0]], first[run[-1]] + cnt[rank][run[-1]]
        q.dma_start(T.y[:, a:b], T.yb[:, a:b]).then_inc(sem.st, 16)

    runs = []
    for e in sorted(mine):
        if runs and due(e) != EARLY and due(runs[-1][-1]) != EARLY:
            runs[-1].append(e)
        else:
            runs.append([e])
    runs.sort(key=lambda run: max(due(e) for e in run))

    for e in mine:
        if due(e) != NEAR:
            copy(e)
    for run in runs:
        for e in run:
            if due(e) == NEAR:
                copy(e)
        store(g.sync if run is runs[-1] else g.scalar, run)
    g.sync.wait_ge(sem.st, 16 * len(runs))
    g.wait_ge(sem.left, left)
